import numpy as np
import ml_dtypes


def mxq(x, axis, fmt="e4m3"):
    dtype, down = {"e4m3": (ml_dtypes.float8_e4m3fn, 7), "e5m2": (ml_dtypes.float8_e5m2, 14)}[fmt]
    v = np.moveaxis(np.asarray(x, np.float32).astype(ml_dtypes.bfloat16).astype(np.float64), axis, -1)
    blocks = v.reshape(v.shape[:-1] + (-1, 32))
    amax = np.abs(blocks).max(-1, keepdims=True)
    byte = np.maximum(np.where(amax > 0, np.frexp(amax)[1] - 1 + 127, 0) - down, 1)
    scale = np.exp2(byte - 127.0)
    codes = (blocks / scale).astype(np.float32).astype(dtype).astype(np.float64)
    return np.moveaxis((codes * scale).reshape(v.shape), -1, axis)


WIDE = False


def mx_kscale(k):
    if not WIDE:
        return np.ones(k)
    levels = np.array([10, -10, 5, -5, 0])
    if k % 512:
        return np.exp2(np.random.permutation(np.resize(levels, k // 32))).repeat(32)
    a = np.empty((k // 512, 16))
    for p in range(k // 512):
        a[p, :8] = np.random.permutation(np.resize(levels, 8))
        for g in range(8):
            far = levels[np.abs(levels - a[p, g]) >= 10]
            a[p, g + 8] = far[np.random.randint(len(far))]
    return np.exp2(a.ravel()).repeat(32)


def f64(x):
    return np.asarray(x).astype(np.float64)


def striped(idx):
    return np.tile(idx.reshape(-1, 16).T, (8, 1)).astype(np.uint16)


def unstriped(offs):
    return offs[:16].T.reshape(-1).astype(np.int64)


def relu(v):
    return np.maximum(v, 0.0)


K, T, D, S, V, H, N = 512, 2048, 2, 1024, 512, 512, 256


def setup_inputs():
    n = np.random.standard_normal
    s = mx_kscale(K)[:, None]
    u = mx_kscale(H)
    return {
        "xT": (n((K, T)) * s).astype(np.float32),
        "w1": (n((K, H)) / np.sqrt(K) / s * u).astype(np.float32),
        "w2": (n((H, N)) / np.sqrt(H) / u[:, None]).astype(np.float32),
        "gate": np.tile(np.random.uniform(0.2, 1.0, (D, 1, V)) / np.sqrt(D), (1, N, 1)).astype(np.float32),
        "offs": striped(np.random.permutation(T)[:S]),
        "pos1": striped(np.random.permutation(S)[:V]),
        "pos2": striped(np.random.permutation(S)[:V]),
    }


def reference(xT, w1, w2, gate, offs, pos1, pos2):
    idx = unstriped(offs)
    xq = mxq(f64(xT)[:, idx], 0, "e4m3")
    h = relu(mxq(f64(w1), 0, "e4m3").T @ xq)
    y = mxq(f64(w2), 0, "e4m3").T @ mxq(h, 0, "e4m3")
    return sum(f64(gate[d]) * y[:, unstriped(p)] for d, p in enumerate((pos1, pos2)))

@@ -1,0 +1,234 @@
+from contextlib import ExitStack
+
+import concourse.mybir as mybir
+
+K, T, S, H, N, V = 512, 2048, 1024, 512, 256, 512
+P = 128
+
+F32 = mybir.dt.float32
+BF16 = mybir.dt.bfloat16
+U32 = mybir.dt.uint32
+U16 = mybir.dt.uint16
+U8 = mybir.dt.uint8
+FP8X4 = mybir.dt.float8_e4m3fn_x4
+
+COPY = mybir.ActivationFunctionType.Copy
+RELU = mybir.ActivationFunctionType.Relu
+MULT = mybir.AluOpType.mult
+ADD = mybir.AluOpType.add
+MAX = mybir.AluOpType.max
+
+FLOPS = 2 * S * H * K + 2 * S * N * H
+
+
+def tile_picked_sub_mlp_relu_sub_e_kernel(tc, xT, w1, w2, gate, offs, pos1, pos2, out):
+    nc = tc.nc
+    with ExitStack() as ctx:
+        keep = ctx.enter_context(tc.tile_pool(name="keep", bufs=1))
+        hbank = ctx.enter_context(tc.psum_pool(name="hbank", bufs=4))
+        ybank = ctx.enter_context(tc.psum_pool(name="ybank", bufs=1))
+
+        offs_t = keep.tile([P, S // 16], U16, name="offs_t")
+        pos_t = [keep.tile([P, V // 16], U16, name=f"pos_t{d}") for d in range(2)]
+        raw = [keep.tile([P, 2, T], F32, name=f"raw{u}", align_bytes=64) for u in range(2)]
+        xb = [keep.tile([P, T, 2], BF16, name=f"xb{u}", align_bytes=64) for u in range(2)]
+        xg = keep.tile([P, S, 4], BF16, name="xg", align_bytes=64)
+        xc = keep.tile([P, S], U32, name="xc", align_bytes=64)
+        xs = keep.tile([P, S], U8, name="xs", align_bytes=64)
+        w1r = keep.tile([P, 4, H], F32, name="w1r", align_bytes=64)
+        w1g = keep.tile([P, 4, P, 4], BF16, name="w1g", align_bytes=64)
+        w1c = keep.tile([P, H], U32, name="w1c", align_bytes=64)
+        w1s = keep.tile([P, H], U8, name="w1s", align_bytes=64)
+        w2r = keep.tile([P, 4, N], F32, name="w2r", align_bytes=64)
+        w2g = keep.tile([P, N, 4], BF16, name="w2g", align_bytes=64)
+        w2c = keep.tile([P, N], U32, name="w2c", align_bytes=64)
+        w2s = keep.tile([P, N], U8, name="w2s", align_bytes=64)
+        hg = keep.tile([P, S, 4], BF16, name="hg", align_bytes=64)
+        hc = keep.tile([P, S], U32, name="hc", align_bytes=64)
+        hs = keep.tile([P, S], U8, name="hs", align_bytes=64)
+        y = [keep.tile([P, S], F32, name=f"y{m}", align_bytes=64) for m in range(2)]
+        gt = [[keep.tile([P, V], F32, name=f"gt{m}{d}", align_bytes=64) for d in range(2)] for m in range(2)]
+        part = [[keep.tile([P, V], F32, name=f"part{m}{d}", align_bytes=64) for d in range(2)] for m in range(2)]
+        res = [keep.tile([P, V], F32, name=f"res{m}", align_bytes=64) for m in range(2)]
+        warm = keep.tile([P, 8], F32, name="warm")
+
+        x4 = xT.rearrange("(p j) t -> p j t", j=4)
+        x_chunks = [[(0, 1024), (1024, 2048)], [(0, 1024), (1024, 1536), (1536, 2048)]]
+
+        def load_x(u, a, b):
+            nc.sync.dma_start(out=raw[u][:, :, a:b], in_=x4[:, 2 * u : 2 * u + 2, a:b])
+
+        for a, b in x_chunks[0]:
+            load_x(0, a, b)
+        nc.sync.dma_start(out=offs_t[:], in_=offs)
+        for a, b in x_chunks[1]:
+            load_x(1, a, b)
+        w1v = w1.rearrange("(p j) c -> p j c", j=4)
+        for a in (0, 256):
+            nc.sync.dma_start(out=w1r[:, :, a : a + 256], in_=w1v[:, :, a : a + 256])
+        w2v = w2.rearrange("(g t r) n -> t g r n", t=4, r=8)
+        for t in range(4):
+            nc.sync.dma_start(out=w2r[:, t, :], in_=w2v[t])
+        nc.sync.dma_start(out=pos_t[0][:], in_=pos1)
+        nc.sync.dma_start(out=pos_t[1][:], in_=pos2)
+        for m in range(2):
+            for d in range(2):
+                nc.sync.dma_start(out=gt[m][d][:], in_=gate[d, m * P : (m + 1) * P, :])
+
+        nc.vector.memset(warm[:], 0.0)
+        nc.scalar.activation(warm[:, 0:4], warm[:, 4:8], RELU)
+
+        def cast_x(engine, u, a, b):
+            dst = xb[u][:, a:b, :]
+            src = raw[u][:, :, a:b].rearrange("p e t -> p t e")
+            if engine == "v":
+                nc.vector.tensor_copy(dst, src)
+            else:
+                nc.scalar.copy(dst, src)
+
+        def gather_x(u, a, b):
+            words = xg[:].rearrange("p n j -> p (n j)").bitcast(U32)
+            window = xb[u][:].rearrange("p t e -> p (t e)").bitcast(U32)
+            nc.vector.tensor_copy(words[:, 2 * a + u : 2 * b : 2], window.indirect(offs_t[:, a // 16 : b // 16]))
+
+        def quant(codes, scales, grouped, a, b):
+            nc.vector.quantize_mx(out=codes[:, a:b].bitcast(FP8X4), scales=scales[:, a:b], in_=grouped[:, 4 * a : 4 * b])
+
+        xflat = xg[:].rearrange("p n j -> p (n j)")
+        hflat = hg[:].rearrange("p n j -> p (n j)")
+
+
+        w1src = w1r[:].rearrange("p j (g t r) -> p t g r j", t=4, r=8)
+        w1dst = w1g[:].rearrange("p t (g r) j -> p t g r j", r=8)
+        w1flat = w1g[:].rearrange("p t m j -> p (t m j)")
+        w2src = w2r[:].rearrange("p t n -> p n t")
+
+        def cast_w1(engine, half, t):
+            gs = slice(8 * half, 8 * half + 8)
+            if engine == "s":
+                nc.scalar.copy(w1dst[:, t, gs], w1src[:, t, gs])
+            elif engine == "v":
+                nc.vector.tensor_copy(w1dst[:, t, gs], w1src[:, t, gs])
+            else:
+                nc.gpsimd.tensor_scalar(w1dst[:, t, gs], w1src[:, t, gs], 1.0, 0.0, MULT, ADD)
+
+        def cast_w2(a, b):
+            nc.gpsimd.tensor_scalar(w2g[:, a:b], w2src[:, a:b], 1.0, 0.0, MULT, ADD)
+
+        yb = [[ybank.tile([P, 512], F32, name=f"yb{m}{hf}") for hf in range(2)] for m in range(2)]
+
+        def layer1(c, engine):
+            bank = hbank.tile([P, 4, P], F32, name="hb")
+            for t in range(4):
+                nc.tensor.matmul_mx(
+                    out=bank[:, t, :],
+                    lhsT=w1c[:, t * P : (t + 1) * P].bitcast(FP8X4),
+                    lhsT_scale=w1s[:, t * P : (t + 1) * P],
+                    rhs=xc[:, c * P : (c + 1) * P].bitcast(FP8X4),
+                    rhs_scale=xs[:, c * P : (c + 1) * P],
+                    start=True,
+                    stop=True,
+                )
+            dst = hg[:, c * P : (c + 1) * P, :]
+            src = bank[:].rearrange("p t n -> p n t")
+            if engine == "v":
+                nc.vector.tensor_scalar(dst, src, 0.0, None, MAX)
+            else:
+                nc.scalar.activation(dst, src, RELU)
+
+        def layer2(m, a, b):
+            nc.tensor.matmul_mx(
+                out=yb[m][a // 512][:, a % 512 : a % 512 + b - a],
+                lhsT=w2c[:, m * P : (m + 1) * P].bitcast(FP8X4),
+                lhsT_scale=w2s[:, m * P : (m + 1) * P],
+                rhs=hc[:, a:b].bitcast(FP8X4),
+                rhs_scale=hs[:, a:b],
+                start=True,
+                stop=True,
+            )
+
+        def copy_y(engine, m, a, b):
+            dst = y[m][:, a:b]
+            src = yb[m][a // 512][:, a % 512 : a % 512 + b - a]
+            if engine == "v":
+                nc.vector.tensor_copy(dst, src)
+            else:
+                nc.scalar.copy(dst, src)
+
+        def gather_y(m, d, a, b):
+            idx = pos_t[d][:] if b - a == V else pos_t[d][:, a // 16 : b // 16]
+            nc.vector.tensor_tensor(part[m][d][:, a:b], y[m][:].indirect(idx), gt[m][d][:, a:b], MULT)
+
+        def finish(m, a, b):
+            nc.vector.tensor_tensor(res[m][:, a:b], part[m][0][:, a:b], part[m][1][:, a:b], ADD)
+            nc.sync.dma_start(out=out[m * P : (m + 1) * P, a:b], in_=res[m][:, a:b])
+
+        cast_x("s", 0, 0, 576)
+        cast_x("v", 0, 576, 1024)
+        cast_x("s", 0, 1024, 1536)
+        cast_x("v", 0, 1536, 2048)
+        gather_x(0, 0, 512)
+        cast_x("s", 1, 0, 576)
+        cast_x("v", 1, 576, 1024)
+        gather_x(0, 512, 1024)
+        cast_x("s", 1, 1024, 1216)
+        cast_x("v", 1, 1216, 1536)
+        cast_x("s", 1, 1536, 1728)
+        cast_x("v", 1, 1728, 2048)
+        cast_w1("g", 0, 2)
+        cast_w1("s", 0, 0)
+        cast_w1("g", 0, 3)
+        cast_w1("s", 0, 1)
+        gather_x(1, 0, 512)
+        cast_w1("g", 1, 2)
+        cast_w1("s", 1, 0)
+        cast_w1("g", 1, 3)
+        cast_w1("s", 1, 1)
+        gather_x(1, 512, 1024)
+        quant(xc, xs, xflat, 0, 256)
+        quant(w1c, w1s, w1flat, 0, 128)
+        quant(w1c, w1s, w1flat, 128, 256)
+        quant(w1c, w1s, w1flat, 256, 384)
+        quant(w1c, w1s, w1flat, 384, 512)
+        cast_w2(0, 128)
+        cast_w2(128, 256)
+        layer1(0, "s")
+        layer1(1, "v")
+        quant(xc, xs, xflat, 256, 512)
+        quant(xc, xs, xflat, 512, 1024)
+        layer1(2, "s")
+        layer1(3, "v")
+        layer1(4, "s")
+        quant(hc, hs, hflat, 0, 256)
+        layer1(5, "s")
+        quant(hc, hs, hflat, 256, 512)
+        layer1(6, "v")
+        layer1(7, "s")
+        quant(w2c, w2s, w2g[:].rearrange("p n j -> p (n j)"), 0, 256)
+        layer2(0, 0, 256)
+        layer2(1, 0, 256)
+        layer2(0, 256, 512)
+        layer2(1, 256, 512)
+        quant(hc, hs, hflat, 512, 768)
+        copy_y("s", 0, 0, 512)
+        layer2(0, 512, 768)
+        layer2(1, 512, 768)
+        quant(hc, hs, hflat, 768, 896)
+        quant(hc, hs, hflat, 896, 1024)
+        copy_y("v", 0, 512, 768)
+        layer2(0, 768, 896)
+        layer2(0, 896, 1024)
+        layer2(1, 768, 896)
+        layer2(1, 896, 1024)
+        copy_y("v", 0, 768, 1024)
+        copy_y("s", 1, 0, 512)
+        copy_y("s", 1, 512, 1024)
+        gather_y(0, 0, 0, 512)
+        gather_y(0, 1, 0, 512)
+        finish(0, 0, 512)
+        gather_y(1, 0, 0, 384)
+        gather_y(1, 1, 0, 384)
+        finish(1, 0, 384)
+        gather_y(1, 0, 384, 512)
+        gather_y(1, 1, 384, 512)
+        finish(1, 384, 512)

@@ -53,19 +53,17 @@ def tile_picked_sub_mlp_relu_sub_e_kernel(tc, xT, w1, w2, gate, offs, pos1, pos2
         warm = keep.tile([P, 8], F32, name="warm")
 
         x4 = xT.rearrange("(p j) t -> p j t", j=4)
-        x_chunks = [[(0, 1024), (1024, 2048)], [(0, 1024), (1024, 1536), (1536, 2048)]]
 
         def load_x(u, a, b):
             nc.sync.dma_start(out=raw[u][:, :, a:b], in_=x4[:, 2 * u : 2 * u + 2, a:b])
 
-        for a, b in x_chunks[0]:
-            load_x(0, a, b)
+        load_x(0, 0, 1024)
+        load_x(0, 1024, 2048)
         nc.sync.dma_start(out=offs_t[:], in_=offs)
-        for a, b in x_chunks[1]:
-            load_x(1, a, b)
-        w1v = w1.rearrange("(p j) c -> p j c", j=4)
-        for a in (0, 256):
-            nc.sync.dma_start(out=w1r[:, :, a : a + 256], in_=w1v[:, :, a : a + 256])
+        load_x(1, 0, 1024)
+        nc.sync.dma_start(out=w1r[:], in_=w1.rearrange("(p j) c -> p j c", j=4))
+        load_x(1, 1024, 1536)
+        load_x(1, 1536, 2048)
         w2v = w2.rearrange("(g t r) n -> t g r n", t=4, r=8)
         for t in range(4):
             nc.sync.dma_start(out=w2r[:, t, :], in_=w2v[t])
@@ -100,25 +98,29 @@ def tile_picked_sub_mlp_relu_sub_e_kernel(tc, xT, w1, w2, gate, offs, pos1, pos2
 
         w1src = w1r[:].rearrange("p j (g t r) -> p t g r j", t=4, r=8)
         w1dst = w1g[:].rearrange("p t (g r) j -> p t g r j", r=8)
+        w2flat = w2g[:].rearrange("p n j -> p (n j)")
         w1flat = w1g[:].rearrange("p t m j -> p (t m j)")
         w2src = w2r[:].rearrange("p t n -> p n t")
 
-        def cast_w1(engine, half, t):
-            gs = slice(8 * half, 8 * half + 8)
+        def cast_w1(engine, t):
             if engine == "s":
-                nc.scalar.copy(w1dst[:, t, gs], w1src[:, t, gs])
-            elif engine == "v":
-                nc.vector.tensor_copy(w1dst[:, t, gs], w1src[:, t, gs])
+                nc.scalar.copy(w1dst[:, t], w1src[:, t])
             else:
-                nc.gpsimd.tensor_scalar(w1dst[:, t, gs], w1src[:, t, gs], 1.0, 0.0, MULT, ADD)
+                nc.vector.tensor_copy(w1dst[:, t], w1src[:, t])
 
-        def cast_w2(a, b):
+        def cast_w2(engine, a, b):
+            if engine == "s":
+                nc.scalar.copy(w2g[:, a:b], w2src[:, a:b])
+                return
             nc.gpsimd.tensor_scalar(w2g[:, a:b], w2src[:, a:b], 1.0, 0.0, MULT, ADD)
 
         yb = [[ybank.tile([P, 512], F32, name=f"yb{m}{hf}") for hf in range(2)] for m in range(2)]
 
-        def layer1(c, engine):
+        banks = {}
+
+        def layer1(c):
             bank = hbank.tile([P, 4, P], F32, name="hb")
+            banks[c] = bank
             for t in range(4):
                 nc.tensor.matmul_mx(
                     out=bank[:, t, :],
@@ -129,8 +131,10 @@ def tile_picked_sub_mlp_relu_sub_e_kernel(tc, xT, w1, w2, gate, offs, pos1, pos2
                     start=True,
                     stop=True,
                 )
+
+        def relu_h(engine, c):
             dst = hg[:, c * P : (c + 1) * P, :]
-            src = bank[:].rearrange("p t n -> p n t")
+            src = banks[c][:].rearrange("p t n -> p n t")
             if engine == "v":
                 nc.vector.tensor_scalar(dst, src, 0.0, None, MAX)
             else:
@@ -163,72 +167,75 @@ def tile_picked_sub_mlp_relu_sub_e_kernel(tc, xT, w1, w2, gate, offs, pos1, pos2
             nc.vector.tensor_tensor(res[m][:, a:b], part[m][0][:, a:b], part[m][1][:, a:b], ADD)
             nc.sync.dma_start(out=out[m * P : (m + 1) * P, a:b], in_=res[m][:, a:b])
 
-        cast_x("s", 0, 0, 576)
-        cast_x("v", 0, 576, 1024)
-        cast_x("s", 0, 1024, 1536)
-        cast_x("v", 0, 1536, 2048)
-        gather_x(0, 0, 512)
-        cast_x("s", 1, 0, 576)
-        cast_x("v", 1, 576, 1024)
+        cast_x("s", 0, 1024, 1344)
+        cast_x("s", 0, 0, 512)
+        cast_x("s", 1, 1024, 1152)
+        cast_x("v", 0, 1344, 2048)
+        cast_x("v", 1, 512, 1024)
+        cast_x("v", 0, 512, 1024)
+        cast_w2("s", 0, 128)
+        cast_x("s", 1, 0, 512)
+        cast_w2("s", 128, 256)
+        cast_w1("v", 0)
+        cast_x("s", 1, 1536, 1664)
+        cast_w1("v", 3)
         gather_x(0, 512, 1024)
-        cast_x("s", 1, 1024, 1216)
-        cast_x("v", 1, 1216, 1536)
-        cast_x("s", 1, 1536, 1728)
-        cast_x("v", 1, 1728, 2048)
-        cast_w1("g", 0, 2)
-        cast_w1("s", 0, 0)
-        cast_w1("g", 0, 3)
-        cast_w1("s", 0, 1)
-        gather_x(1, 0, 512)
-        cast_w1("g", 1, 2)
-        cast_w1("s", 1, 0)
-        cast_w1("g", 1, 3)
-        cast_w1("s", 1, 1)
-        gather_x(1, 512, 1024)
-        quant(xc, xs, xflat, 0, 256)
-        quant(w1c, w1s, w1flat, 0, 128)
-        quant(w1c, w1s, w1flat, 128, 256)
-        quant(w1c, w1s, w1flat, 256, 384)
-        quant(w1c, w1s, w1flat, 384, 512)
-        cast_w2(0, 128)
-        cast_w2(128, 256)
-        layer1(0, "s")
-        layer1(1, "v")
+        cast_x("v", 1, 1152, 1536)
+        gather_x(0, 0, 512)
+        cast_x("v", 1, 1664, 2048)
+        gather_x(1, 256, 512)
+        cast_w1("s", 2)
+        gather_x(1, 512, 768)
+        cast_w1("v", 1)
         quant(xc, xs, xflat, 256, 512)
-        quant(xc, xs, xflat, 512, 1024)
-        layer1(2, "s")
-        layer1(3, "v")
-        layer1(4, "s")
-        quant(hc, hs, hflat, 0, 256)
-        layer1(5, "s")
+        quant(w1c, w1s, w1flat, 0, 512)
+        gather_x(1, 768, 1024)
+        quant(xc, xs, xflat, 768, 1024)
+        quant(xc, xs, xflat, 512, 768)
+        layer1(2)
+        layer1(3)
+        gather_x(1, 0, 256)
+        quant(xc, xs, xflat, 0, 256)
+        layer1(5)
+        relu_h("s", 3)
+        layer1(7)
+        relu_h("v", 5)
+        layer1(4)
+        relu_h("v", 4)
+        quant(w2c, w2s, w2flat, 0, 256)
+        relu_h("s", 2)
+        layer1(6)
+        quant(hc, hs, hflat, 512, 768)
+        relu_h("s", 7)
+        relu_h("s", 6)
+        layer1(1)
+        relu_h("s", 1)
+        quant(hc, hs, hflat, 768, 896)
+        layer1(0)
+        relu_h("v", 0)
         quant(hc, hs, hflat, 256, 512)
-        layer1(6, "v")
-        layer1(7, "s")
-        quant(w2c, w2s, w2g[:].rearrange("p n j -> p (n j)"), 0, 256)
+        layer2(1, 256, 512)
+        quant(hc, hs, hflat, 0, 256)
+        quant(hc, hs, hflat, 896, 1024)
+        layer2(0, 256, 512)
+        layer2(1, 896, 1024)
         layer2(0, 0, 256)
         layer2(1, 0, 256)
-        layer2(0, 256, 512)
-        layer2(1, 256, 512)
-        quant(hc, hs, hflat, 512, 768)
-        copy_y("s", 0, 0, 512)
-        layer2(0, 512, 768)
-        layer2(1, 512, 768)
-        quant(hc, hs, hflat, 768, 896)
-        quant(hc, hs, hflat, 896, 1024)
-        copy_y("v", 0, 512, 768)
-        layer2(0, 768, 896)
         layer2(0, 896, 1024)
-        layer2(1, 768, 896)
-        layer2(1, 896, 1024)
-        copy_y("v", 0, 768, 1024)
+        layer2(0, 768, 896)
+        layer2(1, 512, 768)
         copy_y("s", 1, 0, 512)
+        layer2(0, 512, 768)
+        layer2(1, 768, 896)
+        copy_y("s", 0, 512, 1024)
         copy_y("s", 1, 512, 1024)
+        copy_y("v", 0, 0, 512)
         gather_y(0, 0, 0, 512)
         gather_y(0, 1, 0, 512)
-        finish(0, 0, 512)
         gather_y(1, 0, 0, 384)
+        finish(0, 0, 512)
         gather_y(1, 1, 0, 384)
-        finish(1, 0, 384)
         gather_y(1, 0, 384, 512)
         gather_y(1, 1, 384, 512)
+        finish(1, 0, 384)
         finish(1, 384, 512)

@@ -30,8 +30,10 @@ def tile_picked_sub_mlp_relu_sub_e_kernel(tc, xT, w1, w2, gate, offs, pos1, pos2
 
         offs_t = keep.tile([P, S // 16], U16, name="offs_t")
         pos_t = [keep.tile([P, V // 16], U16, name=f"pos_t{d}") for d in range(2)]
-        raw = [keep.tile([P, 2, T], F32, name=f"raw{u}", align_bytes=64) for u in range(2)]
-        xb = [keep.tile([P, T, 2], BF16, name=f"xb{u}", align_bytes=64) for u in range(2)]
+        raw = keep.tile([P, 2, T], F32, name="raw", align_bytes=64)
+        rawp = {t: keep.tile([P, T], F32, name=f"rawp{t}", align_bytes=64) for t in (2, 3)}
+        xb = keep.tile([P, T, 2], BF16, name="xb", align_bytes=64)
+        pb = {t: keep.tile([P, T], BF16, name=f"pb{t}", align_bytes=64) for t in (2, 3)}
         xg = keep.tile([P, S, 4], BF16, name="xg", align_bytes=64)
         xc = keep.tile([P, S], U32, name="xc", align_bytes=64)
         xs = keep.tile([P, S], U8, name="xs", align_bytes=64)
@@ -53,17 +55,13 @@ def tile_picked_sub_mlp_relu_sub_e_kernel(tc, xT, w1, w2, gate, offs, pos1, pos2
         warm = keep.tile([P, 8], F32, name="warm")
 
         x4 = xT.rearrange("(p j) t -> p j t", j=4)
-
-        def load_x(u, a, b):
-            nc.sync.dma_start(out=raw[u][:, :, a:b], in_=x4[:, 2 * u : 2 * u + 2, a:b])
-
-        load_x(0, 0, 1024)
-        load_x(0, 1024, 2048)
+        for a in (0, 1024):
+            nc.sync.dma_start(out=raw[:, :, a : a + 1024], in_=x4[:, 0:2, a : a + 1024])
         nc.sync.dma_start(out=offs_t[:], in_=offs)
-        load_x(1, 0, 1024)
+        nc.sync.dma_start(out=rawp[2][:], in_=x4[:, 2, :])
         nc.sync.dma_start(out=w1r[:], in_=w1.rearrange("(p j) c -> p j c", j=4))
-        load_x(1, 1024, 1536)
-        load_x(1, 1536, 2048)
+        for a in (0, 1024):
+            nc.sync.dma_start(out=rawp[3][:, a : a + 1024], in_=x4[:, 3, a : a + 1024])
         w2v = w2.rearrange("(g t r) n -> t g r n", t=4, r=8)
         for t in range(4):
             nc.sync.dma_start(out=w2r[:, t, :], in_=w2v[t])
@@ -76,46 +74,48 @@ def tile_picked_sub_mlp_relu_sub_e_kernel(tc, xT, w1, w2, gate, offs, pos1, pos2
         nc.vector.memset(warm[:], 0.0)
         nc.scalar.activation(warm[:, 0:4], warm[:, 4:8], RELU)
 
-        def cast_x(engine, u, a, b):
-            dst = xb[u][:, a:b, :]
-            src = raw[u][:, :, a:b].rearrange("p e t -> p t e")
-            if engine == "v":
-                nc.vector.tensor_copy(dst, src)
-            else:
+        def copy(engine, dst, src):
+            if engine == "s":
                 nc.scalar.copy(dst, src)
+            else:
+                nc.vector.tensor_copy(dst, src)
+
+        def cast_x(engine, u, a, b):
+            copy(engine, xb[:, a:b, :], raw[:, :, a:b].rearrange("p e t -> p t e"))
+
+        def cast_p(engine, t, a, b):
+            copy(engine, pb[t][:, a:b], rawp[t][:, a:b])
+
+        xwords = xg[:].rearrange("p n j -> p (n j)").bitcast(U32)
+        xwindow = xb[:].rearrange("p t e -> p (t e)").bitcast(U32)
 
         def gather_x(u, a, b):
-            words = xg[:].rearrange("p n j -> p (n j)").bitcast(U32)
-            window = xb[u][:].rearrange("p t e -> p (t e)").bitcast(U32)
-            nc.vector.tensor_copy(words[:, 2 * a + u : 2 * b : 2], window.indirect(offs_t[:, a // 16 : b // 16]))
+            nc.vector.tensor_copy(xwords[:, 2 * a : 2 * b : 2], xwindow.indirect(offs_t[:, a // 16 : b // 16]))
+
+        def gather_v(t, a, b):
+            nc.vector.tensor_copy(xg[:, a:b, t], rawp[t][:].indirect(offs_t[:, a // 16 : b // 16]))
+
+        def gather_s(t, a, b):
+            nc.scalar.activation(xg[:, a:b, t], pb[t][:].indirect(offs_t[:, a // 16 : b // 16]), COPY)
 
         def quant(codes, scales, grouped, a, b):
             nc.vector.quantize_mx(out=codes[:, a:b].bitcast(FP8X4), scales=scales[:, a:b], in_=grouped[:, 4 * a : 4 * b])
 
         xflat = xg[:].rearrange("p n j -> p (n j)")
         hflat = hg[:].rearrange("p n j -> p (n j)")
-
-
         w1src = w1r[:].rearrange("p j (g t r) -> p t g r j", t=4, r=8)
         w1dst = w1g[:].rearrange("p t (g r) j -> p t g r j", r=8)
-        w2flat = w2g[:].rearrange("p n j -> p (n j)")
         w1flat = w1g[:].rearrange("p t m j -> p (t m j)")
         w2src = w2r[:].rearrange("p t n -> p n t")
+        w2flat = w2g[:].rearrange("p n j -> p (n j)")
 
         def cast_w1(engine, t):
-            if engine == "s":
-                nc.scalar.copy(w1dst[:, t], w1src[:, t])
-            else:
-                nc.vector.tensor_copy(w1dst[:, t], w1src[:, t])
+            copy(engine, w1dst[:, t], w1src[:, t])
 
         def cast_w2(engine, a, b):
-            if engine == "s":
-                nc.scalar.copy(w2g[:, a:b], w2src[:, a:b])
-                return
-            nc.gpsimd.tensor_scalar(w2g[:, a:b], w2src[:, a:b], 1.0, 0.0, MULT, ADD)
+            copy(engine, w2g[:, a:b], w2src[:, a:b])
 
         yb = [[ybank.tile([P, 512], F32, name=f"yb{m}{hf}") for hf in range(2)] for m in range(2)]
-
         banks = {}
 
         def layer1(c):
@@ -128,6 +128,20 @@ def tile_picked_sub_mlp_relu_sub_e_kernel(tc, xT, w1, w2, gate, offs, pos1, pos2
                     lhsT_scale=w1s[:, t * P : (t + 1) * P],
                     rhs=xc[:, c * P : (c + 1) * P].bitcast(FP8X4),
                     rhs_scale=xs[:, c * P : (c + 1) * P],
+                    start=True,
+                    stop=True,
+                )
+
+        def warm_pe():
+            bank = hbank.tile([P, 4, P], F32, name="hb")
+            flat = bank[:].rearrange("p t n -> p (t n)")
+            for n in (512, 512, 256):
+                nc.tensor.matmul_mx(
+                    out=flat[:, 0:n],
+                    lhsT=w1c[:, 0:P].bitcast(FP8X4),
+                    lhsT_scale=w1s[:, 0:P],
+                    rhs=w1c[:, 0:n].bitcast(FP8X4),
+                    rhs_scale=w1s[:, 0:n],
                     start=True,
                     stop=True,
                 )
@@ -152,12 +166,7 @@ def tile_picked_sub_mlp_relu_sub_e_kernel(tc, xT, w1, w2, gate, offs, pos1, pos2
             )
 
         def copy_y(engine, m, a, b):
-            dst = y[m][:, a:b]
-            src = yb[m][a // 512][:, a % 512 : a % 512 + b - a]
-            if engine == "v":
-                nc.vector.tensor_copy(dst, src)
-            else:
-                nc.scalar.copy(dst, src)
+            copy(engine, y[m][:, a:b], yb[m][a // 512][:, a % 512 : a % 512 + b - a])
 
         def gather_y(m, d, a, b):
             idx = pos_t[d][:] if b - a == V else pos_t[d][:, a // 16 : b // 16]
@@ -167,69 +176,63 @@ def tile_picked_sub_mlp_relu_sub_e_kernel(tc, xT, w1, w2, gate, offs, pos1, pos2
             nc.vector.tensor_tensor(res[m][:, a:b], part[m][0][:, a:b], part[m][1][:, a:b], ADD)
             nc.sync.dma_start(out=out[m * P : (m + 1) * P, a:b], in_=res[m][:, a:b])
 
-        cast_x("s", 0, 1024, 1344)
-        cast_x("s", 0, 0, 512)
-        cast_x("s", 1, 1024, 1152)
-        cast_x("v", 0, 1344, 2048)
-        cast_x("v", 1, 512, 1024)
-        cast_x("v", 0, 512, 1024)
-        cast_w2("s", 0, 128)
-        cast_x("s", 1, 0, 512)
-        cast_w2("s", 128, 256)
-        cast_w1("v", 0)
-        cast_x("s", 1, 1536, 1664)
-        cast_w1("v", 3)
-        gather_x(0, 512, 1024)
-        cast_x("v", 1, 1152, 1536)
+        cast_x("s", 0, 0, 576)
+        cast_x("v", 0, 576, 1024)
+        cast_x("s", 0, 1024, 1408)
+        cast_x("v", 0, 1408, 2048)
         gather_x(0, 0, 512)
-        cast_x("v", 1, 1664, 2048)
-        gather_x(1, 256, 512)
-        cast_w1("s", 2)
-        gather_x(1, 512, 768)
+        gather_x(0, 512, 1024)
+        cast_p("s", 2, 0, 2048)
+        gather_v(2, 0, 512)
+        gather_s(2, 512, 1024)
+        cast_w1("v", 0)
         cast_w1("v", 1)
-        quant(xc, xs, xflat, 256, 512)
+        cast_w1("v", 2)
+        cast_w1("v", 3)
         quant(w1c, w1s, w1flat, 0, 512)
-        gather_x(1, 768, 1024)
-        quant(xc, xs, xflat, 768, 1024)
-        quant(xc, xs, xflat, 512, 768)
+        warm_pe()
+        gather_v(3, 0, 256)
+        gather_v(3, 256, 512)
+        cast_p("s", 3, 0, 1024)
+        cast_p("s", 3, 1024, 2048)
+        gather_s(3, 512, 1024)
+        quant(xc, xs, xflat, 0, 256)
+        quant(xc, xs, xflat, 256, 512)
+        layer1(0)
+        layer1(1)
         layer1(2)
         layer1(3)
-        gather_x(1, 0, 256)
-        quant(xc, xs, xflat, 0, 256)
-        layer1(5)
-        relu_h("s", 3)
-        layer1(7)
-        relu_h("v", 5)
-        layer1(4)
-        relu_h("v", 4)
-        quant(w2c, w2s, w2flat, 0, 256)
-        relu_h("s", 2)
-        layer1(6)
-        quant(hc, hs, hflat, 512, 768)
-        relu_h("s", 7)
-        relu_h("s", 6)
-        layer1(1)
-        relu_h("s", 1)
-        quant(hc, hs, hflat, 768, 896)
-        layer1(0)
+        cast_w2("v", 0, 128)
+        cast_w2("v", 128, 256)
         relu_h("v", 0)
-        quant(hc, hs, hflat, 256, 512)
-        layer2(1, 256, 512)
+        relu_h("s", 1)
+        quant(xc, xs, xflat, 512, 768)
+        quant(xc, xs, xflat, 768, 1024)
+        layer1(4)
+        layer1(5)
+        layer1(6)
+        layer1(7)
+        relu_h("s", 2)
+        relu_h("v", 3)
+        quant(w2c, w2s, w2flat, 0, 256)
         quant(hc, hs, hflat, 0, 256)
-        quant(hc, hs, hflat, 896, 1024)
-        layer2(0, 256, 512)
-        layer2(1, 896, 1024)
-        layer2(0, 0, 256)
-        layer2(1, 0, 256)
-        layer2(0, 896, 1024)
-        layer2(0, 768, 896)
-        layer2(1, 512, 768)
-        copy_y("s", 1, 0, 512)
+        relu_h("s", 4)
+        relu_h("s", 5)
+        quant(hc, hs, hflat, 256, 512)
+        layer2(0, 0, 512)
+        relu_h("v", 6)
+        relu_h("s", 7)
+        quant(hc, hs, hflat, 512, 768)
         layer2(0, 512, 768)
-        layer2(1, 768, 896)
-        copy_y("s", 0, 512, 1024)
+        quant(hc, hs, hflat, 768, 1024)
+        layer2(0, 768, 1024)
+        layer2(1, 0, 512)
+        layer2(1, 512, 768)
+        layer2(1, 768, 1024)
+        copy_y("s", 0, 0, 512)
+        copy_y("v", 0, 512, 1024)
+        copy_y("s", 1, 0, 512)
         copy_y("s", 1, 512, 1024)
-        copy_y("v", 0, 0, 512)
         gather_y(0, 0, 0, 512)
         gather_y(0, 1, 0, 512)
         gather_y(1, 0, 0, 384)

@@ -55,8 +55,8 @@ def tile_picked_sub_mlp_relu_sub_e_kernel(tc, xT, w1, w2, gate, offs, pos1, pos2
         warm = keep.tile([P, 8], F32, name="warm")
 
         x4 = xT.rearrange("(p j) t -> p j t", j=4)
-        for a in (0, 1024):
-            nc.sync.dma_start(out=raw[:, :, a : a + 1024], in_=x4[:, 0:2, a : a + 1024])
+        for a, b in ((0, 1024), (1024, 1536), (1536, 2048)):
+            nc.sync.dma_start(out=raw[:, :, a:b], in_=x4[:, 0:2, a:b])
         nc.sync.dma_start(out=offs_t[:], in_=offs)
         nc.sync.dma_start(out=rawp[2][:], in_=x4[:, 2, :])
         nc.sync.dma_start(out=w1r[:], in_=w1.rearrange("(p j) c -> p j c", j=4))
@@ -176,10 +176,12 @@ def tile_picked_sub_mlp_relu_sub_e_kernel(tc, xT, w1, w2, gate, offs, pos1, pos2
             nc.vector.tensor_tensor(res[m][:, a:b], part[m][0][:, a:b], part[m][1][:, a:b], ADD)
             nc.sync.dma_start(out=out[m * P : (m + 1) * P, a:b], in_=res[m][:, a:b])
 
-        cast_x("s", 0, 0, 576)
-        cast_x("v", 0, 576, 1024)
-        cast_x("s", 0, 1024, 1408)
-        cast_x("v", 0, 1408, 2048)
+        cast_x("s", 0, 0, 512)
+        cast_x("v", 0, 512, 1024)
+        cast_x("s", 0, 1024, 1280)
+        cast_x("v", 0, 1280, 1536)
+        cast_x("s", 0, 1536, 1728)
+        cast_x("v", 0, 1728, 2048)
         gather_x(0, 0, 512)
         gather_x(0, 512, 1024)
         cast_p("s", 2, 0, 2048)
@@ -191,18 +193,19 @@ def tile_picked_sub_mlp_relu_sub_e_kernel(tc, xT, w1, w2, gate, offs, pos1, pos2
         cast_w1("v", 3)
         quant(w1c, w1s, w1flat, 0, 512)
         warm_pe()
+        cast_p("s", 3, 0, 1024)
+        cast_p("v", 3, 1024, 2048)
         gather_v(3, 0, 256)
         gather_v(3, 256, 512)
-        cast_p("s", 3, 0, 1024)
-        cast_p("s", 3, 1024, 2048)
-        gather_s(3, 512, 1024)
+        gather_s(3, 512, 768)
+        gather_s(3, 768, 1024)
         quant(xc, xs, xflat, 0, 256)
         quant(xc, xs, xflat, 256, 512)
         layer1(0)
         layer1(1)
         layer1(2)
         layer1(3)
-        cast_w2("v", 0, 128)
+        cast_w2("s", 0, 128)
         cast_w2("v", 128, 256)
         relu_h("v", 0)
         relu_h("s", 1)
@@ -230,7 +233,8 @@ def tile_picked_sub_mlp_relu_sub_e_kernel(tc, xT, w1, w2, gate, offs, pos1, pos2
         layer2(1, 512, 768)
         layer2(1, 768, 1024)
         copy_y("s", 0, 0, 512)
-        copy_y("v", 0, 512, 1024)
+        copy_y("v", 0, 512, 768)
+        copy_y("s", 0, 768, 1024)
         copy_y("s", 1, 0, 512)
         copy_y("s", 1, 512, 1024)
         gather_y(0, 0, 0, 512)

from contextlib import ExitStack

import concourse.mybir as mybir

K, T, S, H, N, V = 512, 2048, 1024, 512, 256, 512
P = 128

F32 = mybir.dt.float32
BF16 = mybir.dt.bfloat16
U32 = mybir.dt.uint32
U16 = mybir.dt.uint16
U8 = mybir.dt.uint8
FP8X4 = mybir.dt.float8_e4m3fn_x4

COPY = mybir.ActivationFunctionType.Copy
RELU = mybir.ActivationFunctionType.Relu
MULT = mybir.AluOpType.mult
ADD = mybir.AluOpType.add
MAX = mybir.AluOpType.max

FLOPS = 2 * S * H * K + 2 * S * N * H


def tile_picked_sub_mlp_relu_sub_e_kernel(tc, xT, w1, w2, gate, offs, pos1, pos2, out):
    nc = tc.nc
    with ExitStack() as ctx:
        keep = ctx.enter_context(tc.tile_pool(name="keep", bufs=1))
        hbank = ctx.enter_context(tc.psum_pool(name="hbank", bufs=4))
        ybank = ctx.enter_context(tc.psum_pool(name="ybank", bufs=1))

        offs_t = keep.tile([P, S // 16], U16, name="offs_t")
        pos_t = [keep.tile([P, V // 16], U16, name=f"pos_t{d}") for d in range(2)]
        raw = keep.tile([P, 2, T], F32, name="raw", align_bytes=64)
        rawp = {t: keep.tile([P, T], F32, name=f"rawp{t}", align_bytes=64) for t in (2, 3)}
        xb = keep.tile([P, T, 2], BF16, name="xb", align_bytes=64)
        pb = {t: keep.tile([P, T], BF16, name=f"pb{t}", align_bytes=64) for t in (2, 3)}
        xg = keep.tile([P, S, 4], BF16, name="xg", align_bytes=64)
        xc = keep.tile([P, S], U32, name="xc", align_bytes=64)
        xs = keep.tile([P, S], U8, name="xs", align_bytes=64)
        w1r = keep.tile([P, 4, H], F32, name="w1r", align_bytes=64)
        w1g = keep.tile([P, 4, P, 4], BF16, name="w1g", align_bytes=64)
        w1c = keep.tile([P, H], U32, name="w1c", align_bytes=64)
        w1s = keep.tile([P, H], U8, name="w1s", align_bytes=64)
        w2r = keep.tile([P, 4, N], F32, name="w2r", align_bytes=64)
        w2g = keep.tile([P, N, 4], BF16, name="w2g", align_bytes=64)
        w2c = keep.tile([P, N], U32, name="w2c", align_bytes=64)
        w2s = keep.tile([P, N], U8, name="w2s", align_bytes=64)
        hg = keep.tile([P, S, 4], BF16, name="hg", align_bytes=64)
        hc = keep.tile([P, S], U32, name="hc", align_bytes=64)
        hs = keep.tile([P, S], U8, name="hs", align_bytes=64)
        y = [keep.tile([P, S], F32, name=f"y{m}", align_bytes=64) for m in range(2)]
        gt = [[keep.tile([P, V], F32, name=f"gt{m}{d}", align_bytes=64) for d in range(2)] for m in range(2)]
        part = [[keep.tile([P, V], F32, name=f"part{m}{d}", align_bytes=64) for d in range(2)] for m in range(2)]
        res = [keep.tile([P, V], F32, name=f"res{m}", align_bytes=64) for m in range(2)]
        warm = keep.tile([P, 8], F32, name="warm")

        x4 = xT.rearrange("(p j) t -> p j t", j=4)
        for a, b in ((0, 1024), (1024, 1536), (1536, 2048)):
            nc.sync.dma_start(out=raw[:, :, a:b], in_=x4[:, 0:2, a:b])
        nc.sync.dma_start(out=offs_t[:], in_=offs)
        nc.sync.dma_start(out=rawp[2][:], in_=x4[:, 2, :])
        nc.sync.dma_start(out=w1r[:], in_=w1.rearrange("(p j) c -> p j c", j=4))
        for a in (0, 1024):
            nc.sync.dma_start(out=rawp[3][:, a : a + 1024], in_=x4[:, 3, a : a + 1024])
        w2v = w2.rearrange("(g t r) n -> t g r n", t=4, r=8)
        for t in range(4):
            nc.sync.dma_start(out=w2r[:, t, :], in_=w2v[t])
        nc.sync.dma_start(out=pos_t[0][:], in_=pos1)
        nc.sync.dma_start(out=pos_t[1][:], in_=pos2)
        for m in range(2):
            for d in range(2):
                nc.sync.dma_start(out=gt[m][d][:], in_=gate[d, m * P : (m + 1) * P, :])

        nc.vector.memset(warm[:], 0.0)
        nc.scalar.activation(warm[:, 0:4], warm[:, 4:8], RELU)

        def copy(engine, dst, src):
            if engine == "s":
                nc.scalar.copy(dst, src)
            else:
                nc.vector.tensor_copy(dst, src)

        def cast_x(engine, u, a, b):
            copy(engine, xb[:, a:b, :], raw[:, :, a:b].rearrange("p e t -> p t e"))

        def cast_p(engine, t, a, b):
            copy(engine, pb[t][:, a:b], rawp[t][:, a:b])

        xwords = xg[:].rearrange("p n j -> p (n j)").bitcast(U32)
        xwindow = xb[:].rearrange("p t e -> p (t e)").bitcast(U32)

        def gather_x(u, a, b):
            nc.vector.tensor_copy(xwords[:, 2 * a : 2 * b : 2], xwindow.indirect(offs_t[:, a // 16 : b // 16]))

        def gather_v(t, a, b):
            nc.vector.tensor_copy(xg[:, a:b, t], rawp[t][:].indirect(offs_t[:, a // 16 : b // 16]))

        def gather_s(t, a, b):
            nc.scalar.activation(xg[:, a:b, t], pb[t][:].indirect(offs_t[:, a // 16 : b // 16]), COPY)

        def quant(codes, scales, grouped, a, b):
            nc.vector.quantize_mx(out=codes[:, a:b].bitcast(FP8X4), scales=scales[:, a:b], in_=grouped[:, 4 * a : 4 * b])

        xflat = xg[:].rearrange("p n j -> p (n j)")
        hflat = hg[:].rearrange("p n j -> p (n j)")
        w1src = w1r[:].rearrange("p j (g t r) -> p t g r j", t=4, r=8)
        w1dst = w1g[:].rearrange("p t (g r) j -> p t g r j", r=8)
        w1flat = w1g[:].rearrange("p t m j -> p (t m j)")
        w2src = w2r[:].rearrange("p t n -> p n t")
        w2flat = w2g[:].rearrange("p n j -> p (n j)")

        def cast_w1(engine, t):
            copy(engine, w1dst[:, t], w1src[:, t])

        def cast_w2(engine, a, b):
            copy(engine, w2g[:, a:b], w2src[:, a:b])

        yb = [[ybank.tile([P, 512], F32, name=f"yb{m}{hf}") for hf in range(2)] for m in range(2)]
        banks = {}

        def layer1(c):
            bank = hbank.tile([P, 4, P], F32, name="hb")
            banks[c] = bank
            for t in range(4):
                nc.tensor.matmul_mx(
                    out=bank[:, t, :],
                    lhsT=w1c[:, t * P : (t + 1) * P].bitcast(FP8X4),
                    lhsT_scale=w1s[:, t * P : (t + 1) * P],
                    rhs=xc[:, c * P : (c + 1) * P].bitcast(FP8X4),
                    rhs_scale=xs[:, c * P : (c + 1) * P],
                    start=True,
                    stop=True,
                )

        def warm_pe():
            bank = hbank.tile([P, 4, P], F32, name="hb")
            flat = bank[:].rearrange("p t n -> p (t n)")
            for n in (512, 512, 256):
                nc.tensor.matmul_mx(
                    out=flat[:, 0:n],
                    lhsT=w1c[:, 0:P].bitcast(FP8X4),
                    lhsT_scale=w1s[:, 0:P],
                    rhs=w1c[:, 0:n].bitcast(FP8X4),
                    rhs_scale=w1s[:, 0:n],
                    start=True,
                    stop=True,
                )

        def relu_h(engine, c):
            dst = hg[:, c * P : (c + 1) * P, :]
            src = banks[c][:].rearrange("p t n -> p n t")
            if engine == "v":
                nc.vector.tensor_scalar(dst, src, 0.0, None, MAX)
            else:
                nc.scalar.activation(dst, src, RELU)

        def layer2(m, a, b):
            nc.tensor.matmul_mx(
                out=yb[m][a // 512][:, a % 512 : a % 512 + b - a],
                lhsT=w2c[:, m * P : (m + 1) * P].bitcast(FP8X4),
                lhsT_scale=w2s[:, m * P : (m + 1) * P],
                rhs=hc[:, a:b].bitcast(FP8X4),
                rhs_scale=hs[:, a:b],
                start=True,
                stop=True,
            )

        def copy_y(engine, m, a, b):
            copy(engine, y[m][:, a:b], yb[m][a // 512][:, a % 512 : a % 512 + b - a])

        def gather_y(m, d, a, b):
            idx = pos_t[d][:] if b - a == V else pos_t[d][:, a // 16 : b // 16]
            nc.vector.tensor_tensor(part[m][d][:, a:b], y[m][:].indirect(idx), gt[m][d][:, a:b], MULT)

        def finish(m, a, b):
            nc.vector.tensor_tensor(res[m][:, a:b], part[m][0][:, a:b], part[m][1][:, a:b], ADD)
            nc.sync.dma_start(out=out[m * P : (m + 1) * P, a:b], in_=res[m][:, a:b])

        cast_x("s", 0, 0, 512)
        cast_x("v", 0, 512, 1024)
        cast_x("s", 0, 1024, 1280)
        cast_x("v", 0, 1280, 1536)
        cast_x("s", 0, 1536, 1728)
        cast_x("v", 0, 1728, 2048)
        gather_x(0, 0, 512)
        gather_x(0, 512, 1024)
        cast_p("s", 2, 0, 2048)
        gather_v(2, 0, 512)
        gather_s(2, 512, 1024)
        cast_w1("v", 0)
        cast_w1("v", 1)
        cast_w1("v", 2)
        cast_w1("v", 3)
        quant(w1c, w1s, w1flat, 0, 512)
        warm_pe()
        cast_p("s", 3, 0, 1024)
        cast_p("v", 3, 1024, 2048)
        gather_v(3, 0, 256)
        gather_v(3, 256, 512)
        gather_s(3, 512, 768)
        gather_s(3, 768, 1024)
        quant(xc, xs, xflat, 0, 256)
        quant(xc, xs, xflat, 256, 512)
        layer1(0)
        layer1(1)
        layer1(2)
        layer1(3)
        cast_w2("s", 0, 128)
        cast_w2("v", 128, 256)
        relu_h("v", 0)
        relu_h("s", 1)
        quant(xc, xs, xflat, 512, 768)
        quant(xc, xs, xflat, 768, 1024)
        layer1(4)
        layer1(5)
        layer1(6)
        layer1(7)
        relu_h("s", 2)
        relu_h("v", 3)
        quant(w2c, w2s, w2flat, 0, 256)
        quant(hc, hs, hflat, 0, 256)
        relu_h("s", 4)
        relu_h("s", 5)
        quant(hc, hs, hflat, 256, 512)
        layer2(0, 0, 512)
        relu_h("v", 6)
        relu_h("s", 7)
        quant(hc, hs, hflat, 512, 768)
        layer2(0, 512, 768)
        quant(hc, hs, hflat, 768, 1024)
        layer2(0, 768, 1024)
        layer2(1, 0, 512)
        layer2(1, 512, 768)
        layer2(1, 768, 1024)
        copy_y("s", 0, 0, 512)
        copy_y("v", 0, 512, 768)
        copy_y("s", 0, 768, 1024)
        copy_y("s", 1, 0, 512)
        copy_y("s", 1, 512, 1024)
        gather_y(0, 0, 0, 512)
        gather_y(0, 1, 0, 512)
        gather_y(1, 0, 0, 384)
        finish(0, 0, 512)
        gather_y(1, 1, 0, 384)
        gather_y(1, 0, 384, 512)
        gather_y(1, 1, 384, 512)
        finish(1, 0, 384)
        finish(1, 384, 512)
